import numpy as np
import ml_dtypes


def mxq(x, axis, fmt="e4m3"):
    dtype, down = {"e4m3": (ml_dtypes.float8_e4m3fn, 7), "e5m2": (ml_dtypes.float8_e5m2, 14)}[fmt]
    v = np.moveaxis(np.asarray(x, np.float32).astype(ml_dtypes.bfloat16).astype(np.float64), axis, -1)
    blocks = v.reshape(v.shape[:-1] + (-1, 32))
    amax = np.abs(blocks).max(-1, keepdims=True)
    byte = np.maximum(np.where(amax > 0, np.frexp(amax)[1] - 1 + 127, 0) - down, 1)
    scale = np.exp2(byte - 127.0)
    codes = (blocks / scale).astype(np.float32).astype(dtype).astype(np.float64)
    return np.moveaxis((codes * scale).reshape(v.shape), -1, axis)


WIDE = False


def mx_kscale(k):
    if not WIDE:
        return np.ones(k)
    levels = np.array([10, -10, 5, -5, 0])
    if k % 512:
        return np.exp2(np.random.permutation(np.resize(levels, k // 32))).repeat(32)
    a = np.empty((k // 512, 16))
    for p in range(k // 512):
        a[p, :8] = np.random.permutation(np.resize(levels, 8))
        for g in range(8):
            far = levels[np.abs(levels - a[p, g]) >= 10]
            a[p, g + 8] = far[np.random.randint(len(far))]
    return np.exp2(a.ravel()).repeat(32)


def f64(x):
    return np.asarray(x).astype(np.float64)


def striped(idx):
    return np.tile(idx.reshape(-1, 16).T, (8, 1)).astype(np.uint16)


def unstriped(offs):
    return offs[:16].T.reshape(-1).astype(np.int64)


def striped8(idx):
    return np.concatenate([x.reshape(-1, 16).T for x in idx]).astype(np.uint16)


def runs(offs, k):
    lists = np.stack([offs[16 * r : 16 * r + 16].T.reshape(-1) for r in range(8)]).astype(np.int64)
    return lists[np.arange(k) % 512 // 64]


def pack_weight(w):
    k, n = w.shape
    w = f64(np.asarray(w, np.float32).astype(ml_dtypes.bfloat16)).reshape(k // 32, 32, n)
    amax = np.abs(w).max(1)
    byte = np.clip(np.where(amax > 0, np.frexp(amax)[1] - 1 + 127 - 7, 1), 1, 254)
    scaled = (w * np.exp2(127.0 - byte)[:, None, :]).reshape(k, n).astype(np.float32)
    words = np.ascontiguousarray(scaled.reshape(k // 512, 128, 4, n).transpose(0, 1, 3, 2)).astype(ml_dtypes.float8_e4m3fn).view(np.uint8)
    return words, np.ascontiguousarray(byte.astype(np.uint8).reshape(k // 512, 16, n))


def unpack_weight(words, scales):
    g, p, n, _ = words.shape
    vals = np.ascontiguousarray(words).view(ml_dtypes.float8_e4m3fn).astype(np.float64) * np.repeat(np.exp2(scales.astype(np.float64) - 127.0), 8, axis=1)[..., None]
    return vals.transpose(0, 1, 3, 2).reshape(g * 512, n)


K, T, S, N, H, J = 512, 2048, 512, 512, 512, 512


def setup_inputs():
    n = np.random.standard_normal
    s = mx_kscale(K)[:, None]
    u = mx_kscale(H)
    packed_xT = pack_weight(n((K, T)) * s)
    return {
        "x_words": packed_xT[0],
        "x_scales": packed_xT[1],
        "w1": (n((K, H)) / np.sqrt(K) / s).astype(np.float32),
        "gn": (np.random.uniform(0.5, 1.5, (H, 1)) * u[:, None]).astype(np.float32),
        "w2": (n((H, N)) / np.sqrt(H) / u[:, None]).astype(np.float32),
        "tab": n((N, J)).astype(np.float32),
        "offs": striped(np.random.permutation(T)[:S]),
        "n1": striped8(np.stack([np.random.permutation(S) for _ in range(8)])),
        "n2": striped8(np.stack([np.random.permutation(S) for _ in range(8)])),
        "n3": striped8(np.random.randint(0, J, (8, S))),
        "n4": striped8(np.random.randint(0, J, (8, S))),
        "n5": striped8(np.stack([np.random.permutation(S) for _ in range(8)])),
    }


def reference(x_words, x_scales, w1, gn, w2, tab, offs, n1, n2, n3, n4, n5):
    xq = unpack_weight(x_words, x_scales)[:, unstriped(offs)]
    y = mxq(f64(w1), 0, "e4m3").T @ xq
    z = f64(gn) * ((np.tanh(y[np.arange(H)[:, None], runs(n1, H)] - y)) * (y[np.arange(H)[:, None], runs(n2, H)]))
    h = mxq(f64(w2), 0, "e4m3").T @ mxq(z, 0, "e4m3")
    return (h[np.arange(N)[:, None], runs(n5, N)]) * (f64(tab)[np.arange(N)[:, None], runs(n3, N)]) + f64(tab)[np.arange(N)[:, None], runs(n4, N)]

@@ -1,0 +1,214 @@
+from contextlib import ExitStack
+
+import concourse.mybir as mybir
+
+K, T, S, N, H = 512, 2048, 512, 512, 512
+FLOPS = 2 * K * H * S + 2 * H * N * S
+
+F32 = mybir.dt.float32
+BF16 = mybir.dt.bfloat16
+I32 = mybir.dt.int32
+U32 = mybir.dt.uint32
+U16 = mybir.dt.uint16
+U8 = mybir.dt.uint8
+FP8X4 = mybir.dt.float8_e4m3fn_x4
+ALU = mybir.AluOpType
+ACT = mybir.ActivationFunctionType
+
+P = 128
+PACK = 4
+HALF = S // 2
+LIST_COLS = S // 16
+SMALLEST_NORMAL = 2.0 ** -126
+
+
+def tile_picked_layfdifkinda_none_p_kernel(tc, x_words, x_scales, w1, gn, w2, tab, offs, n1, n2, n3, n4, n5, out):
+    nc = tc.nc
+    with ExitStack() as ctx:
+        keep = ctx.enter_context(tc.tile_pool(name="keep", bufs=1))
+        psum = ctx.enter_context(tc.psum_pool(name="psum", bufs=1))
+
+        def load_list(name, src):
+            tile = keep.tile([P, LIST_COLS], U16, name=name)
+            nc.sync.dma_start(tile[:], src)
+            return tile
+
+        def half_cols(hf):
+            return slice(hf * HALF, (hf + 1) * HALF)
+
+        def half_list(tile, hf):
+            return tile[:, hf * LIST_COLS // 2 : (hf + 1) * LIST_COLS // 2]
+
+        tab_rows = tab.rearrange("(p t) j -> t p j", t=PACK)
+        out_rows = out.rearrange("(p t) j -> t p j", t=PACK)
+
+        def load_tab(t):
+            tile = keep.tile([P, S], F32, name=f"tab{t}")
+            nc.sync.dma_start(tile[:], tab_rows[t])
+            return tile
+
+        def load_weight_half(name, w, c):
+            tile = keep.tile([P, PACK, HALF], F32, name=f"{name}_raw{c}")
+            nc.sync.dma_start(tile[:], w.rearrange("(p j) n -> p j n", j=PACK)[:, :, half_cols(c)])
+            return tile
+
+        def deal_weight(dealt, raw, c, part, parts):
+            width = HALF // PACK // parts
+            m0 = c * HALF // PACK + part * width
+            nc.scalar.copy(
+                out=dealt[:].rearrange("p (t m j) -> p m j t", t=PACK, j=PACK)[:, m0 : m0 + width],
+                in_=raw[:].rearrange("p j (m t) -> p m j t", t=PACK)[:, part * width : (part + 1) * width],
+            )
+
+        xs = keep.tile([P, T], U8, name="xs", tag="xs")
+        nc.vector.memset(xs[:].bitcast(I32), 0)
+        for q in range(4):
+            nc.sync.dma_start(xs[32 * q : 32 * q + 4, :].bitcast(I32), x_scales[0, 4 * q : 4 * q + 4, :].bitcast(I32))
+
+        gn_sb = keep.tile([P, PACK], F32, name="gn_sb")
+        nc.gpsimd.dma_start(gn_sb[:], gn.rearrange("(p t) o -> p (t o)", t=PACK))
+        n3_sb = load_list("n3_sb", n3)
+        offs_sb = load_list("offs_sb", offs)
+        tab_sb = [load_tab(0)]
+        w1_raw = [load_weight_half("w1", w1, c) for c in range(2)]
+        tab_sb.append(load_tab(1))
+        xw = keep.tile([P, T], I32, name="xw")
+        nc.sync.dma_start(xw[:], x_words[0].rearrange("p c r -> p (c r)").bitcast(I32))
+        tab_sb.append(load_tab(2))
+        n1_sb = load_list("n1_sb", n1)
+        n2_sb = load_list("n2_sb", n2)
+        w2_raw = [load_weight_half("w2", w2, c) for c in range(2)]
+        tab_sb.append(load_tab(3))
+        n5_sb = load_list("n5_sb", n5)
+        n4_sb = load_list("n4_sb", n4)
+
+        factor = {}
+
+        def fetch_factor(t, hf, tag):
+            tile = keep.tile([P, HALF], F32, name=f"factor{t}{hf}", tag=tag)
+            nc.vector.tensor_copy(tile[:], tab_sb[t][:].indirect(half_list(n3_sb, hf)))
+            factor[t, hf] = tile
+
+        gn_safe = keep.tile([P, PACK], F32, name="gn_safe")
+        gn_inv = keep.tile([P, PACK], F32, name="gn_inv")
+        x_scale = keep.tile([P, S], U8, name="x_scale", align_bytes=64)
+        for hf in range(2):
+            fetch_factor(0, hf, f"factor0{hf}")
+        nc.vector.tensor_copy(x_scale[:], xs[:].indirect(offs_sb[:]))
+        gn_abs = keep.tile([P, PACK], F32, name="gn_abs", tag="xs")
+        nc.vector.scalar_tensor_tensor(gn_abs[:], gn_sb[:], -1.0, gn_sb[:], ALU.mult, ALU.max)
+        fetch_factor(1, 0, "factor10")
+        nc.vector.scalar_tensor_tensor(gn_safe[:], gn_abs[:], SMALLEST_NORMAL, gn_sb[:], ALU.is_lt, ALU.add)
+        fetch_factor(1, 1, "factor11")
+        nc.vector.reciprocal(gn_inv[:], gn_safe[:])
+
+        w1_dealt = keep.tile([P, PACK * H], BF16, name="w1_dealt", align_bytes=64)
+        for c in range(2):
+            deal_weight(w1_dealt, w1_raw[c], c, 0, 1)
+        w1_codes = keep.tile([P, H], U32, name="w1_codes", align_bytes=64)
+        w1_scale = keep.tile([P, H], U8, name="w1_scale", align_bytes=64)
+        nc.vector.quantize_mx(out=w1_codes[:].bitcast(FP8X4), scales=w1_scale[:], in_=w1_dealt[:])
+
+        x_codes = keep.tile([P, S], U32, name="x_codes", align_bytes=64)
+        for hf in range(2):
+            nc.vector.tensor_copy(x_codes[:, half_cols(hf)], xw[:].bitcast(U32).indirect(half_list(offs_sb, hf)))
+
+        for hf in range(2):
+            fetch_factor(2, hf, f"factor2{hf}")
+
+        def first_product(bank, t, src_cols, dst_cols):
+            cols = slice(t * P, (t + 1) * P)
+            nc.tensor.matmul_mx(bank[:, dst_cols], w1_codes[:, cols].bitcast(FP8X4), w1_scale[:, cols],
+                                x_codes[:, src_cols].bitcast(FP8X4), x_scale[:, src_cols], start=True, stop=True)
+
+        y_ps = [psum.tile([P, S], F32, name=f"y_ps{t}", tag=f"bank{t}") for t in range(PACK)]
+        y_ps_second = psum.tile([P, S], F32, name="y_ps_second", tag="bank4")
+        gy = [keep.tile([P, S], F32, name=f"gy{t}") for t in range(PACK)]
+        plain = [keep.tile([P, S], F32, name=f"gy_plain{t}") for t in range(PACK)]
+        diff = {}
+
+        def gain(dst, src, t):
+            nc.scalar.activation(dst, src, ACT.Copy, scale=gn_sb[:, t : t + 1])
+
+        def subtract(t):
+            for hf in range(2):
+                d = keep.tile([P, HALF], F32, name=f"diff{t}{hf}")
+                nc.vector.tensor_tensor(d[:], gy[t][:].indirect(half_list(n1_sb, hf)), plain[t][:, half_cols(hf)], ALU.subtract)
+                diff[t, hf] = d
+
+        first_product(y_ps[0], 0, half_cols(0), half_cols(0))
+        first_product(y_ps[1], 1, half_cols(0), half_cols(0))
+        first_product(y_ps_second, 0, half_cols(1), half_cols(1))
+        first_product(y_ps[1], 1, half_cols(1), half_cols(1))
+        for t in range(2, PACK):
+            first_product(y_ps[t], t, slice(0, S), slice(0, S))
+        for hf, bank in enumerate((y_ps[0], y_ps_second)):
+            gain(gy[0][:, half_cols(hf)], bank[:, half_cols(hf)], 0)
+            gain(plain[0][:, half_cols(hf)], bank[:, half_cols(hf)], 0)
+        subtract(0)
+        for t in range(1, PACK):
+            gain(gy[t][:], y_ps[t][:], t)
+            gain(plain[t][:], y_ps[t][:], t)
+            subtract(t)
+
+        th = {}
+        for hf in range(2):
+            for t in range(PACK):
+                tile = keep.tile([P, HALF], F32, name=f"th{t}{hf}", tag=f"th{t}{hf}")
+                nc.scalar.activation(tile[:], diff[t, hf][:], ACT.Tanh, scale=gn_inv[:, t : t + 1])
+                th[t, hf] = tile
+
+        w2_dealt = keep.tile([P, PACK * N], BF16, name="w2_dealt", align_bytes=64)
+        w2_codes = keep.tile([P, N], U32, name="w2_codes", align_bytes=64)
+        w2_scale = keep.tile([P, N], U8, name="w2_scale", align_bytes=64)
+        z32 = [keep.tile([P, PACK, HALF], F32, name=f"z32_{hf}") for hf in range(2)]
+        z16 = [keep.tile([P, PACK * HALF], BF16, name=f"z16_{hf}", align_bytes=64) for hf in range(2)]
+        z_codes = [keep.tile([P, HALF], U32, name=f"z_codes{hf}", align_bytes=64) for hf in range(2)]
+        z_scale = [keep.tile([P, HALF], U8, name=f"z_scale{hf}", align_bytes=64) for hf in range(2)]
+        h_sb = [keep.tile([P, S], F32, name=f"h{t}") for t in range(PACK)]
+
+        def make_z(hf):
+            for t in range(PACK):
+                nc.vector.tensor_tensor(z32[hf][:, t, :], gy[t][:].indirect(half_list(n2_sb, hf)), th[t, hf][:], ALU.mult)
+
+        def weave_z(hf):
+            nc.scalar.copy(
+                out=z16[hf][:].rearrange("p (c i t) -> p c t i", i=4, t=PACK),
+                in_=z32[hf][:].rearrange("p t (c i) -> p c t i", i=4),
+            )
+
+        def quantize_z(hf):
+            nc.vector.quantize_mx(out=z_codes[hf][:].bitcast(FP8X4), scales=z_scale[hf][:], in_=z16[hf][:])
+
+        def second_product(hf):
+            for t in range(PACK):
+                bank = psum.tile([P, S], F32, name=f"h_ps{t}{hf}", tag=f"bank{PACK * (1 - hf) + t}")
+                cols = slice(t * P, (t + 1) * P)
+                nc.tensor.matmul_mx(bank[:, 0:HALF], w2_codes[:, cols].bitcast(FP8X4), w2_scale[:, cols],
+                                    z_codes[hf][:].bitcast(FP8X4), z_scale[hf][:], start=True, stop=True)
+                nc.scalar.copy(h_sb[t][:, half_cols(hf)], bank[:, 0:HALF])
+
+        for part in range(2):
+            deal_weight(w2_dealt, w2_raw[0], 0, part, 2)
+        make_z(0)
+        weave_z(0)
+        for part in range(2):
+            deal_weight(w2_dealt, w2_raw[1], 1, part, 2)
+        make_z(1)
+        weave_z(1)
+        quantize_z(0)
+        nc.vector.quantize_mx(out=w2_codes[:].bitcast(FP8X4), scales=w2_scale[:], in_=w2_dealt[:])
+        second_product(0)
+        fetch_factor(3, 0, "th21")
+        quantize_z(1)
+        fetch_factor(3, 1, "th31")
+        second_product(1)
+
+        for t in range(PACK):
+            prod = [keep.tile([P, HALF], F32, name=f"prod{t}{hf}") for hf in range(2)]
+            res = [keep.tile([P, HALF], F32, name=f"res{t}{hf}") for hf in range(2)]
+            for hf in range(2):
+                nc.vector.tensor_tensor(prod[hf][:], h_sb[t][:].indirect(half_list(n5_sb, hf)), factor[t, hf][:], ALU.mult)
+            for hf in range(2):
+                nc.vector.tensor_tensor(res[hf][:], tab_sb[t][:].indirect(half_list(n4_sb, hf)), prod[hf][:], ALU.add)
+                nc.sync.dma_start(out_rows[t][:, half_cols(hf)], res[hf][:])

@@ -62,17 +62,21 @@ def tile_picked_layfdifkinda_none_p_kernel(tc, x_words, x_scales, w1, gn, w2, ta
 
         xs = keep.tile([P, T], U8, name="xs", tag="xs")
         nc.vector.memset(xs[:].bitcast(I32), 0)
-        for q in range(4):
-            nc.sync.dma_start(xs[32 * q : 32 * q + 4, :].bitcast(I32), x_scales[0, 4 * q : 4 * q + 4, :].bitcast(I32))
 
-        gn_sb = keep.tile([P, PACK], F32, name="gn_sb")
-        nc.gpsimd.dma_start(gn_sb[:], gn.rearrange("(p t) o -> p (t o)", t=PACK))
-        n3_sb = load_list("n3_sb", n3)
-        offs_sb = load_list("offs_sb", offs)
+        def load_scale_rows(queue, q):
+            queue.dma_start(xs[32 * q : 32 * q + 4, :].bitcast(I32), x_scales[0, 4 * q : 4 * q + 4, :].bitcast(I32))
+
         tab_sb = [load_tab(0)]
-        w1_raw = [load_weight_half("w1", w1, c) for c in range(2)]
+        n3_sb = load_list("n3_sb", n3)
+        w1_raw = [load_weight_half("w1", w1, 0)]
         tab_sb.append(load_tab(1))
-        xw = keep.tile([P, T], I32, name="xw")
+        offs_sb = load_list("offs_sb", offs)
+        for q in range(4):
+            load_scale_rows(nc.sync, q)
+        w1_raw.append(load_weight_half("w1", w1, 1))
+        gn_sb = keep.tile([P, PACK], F32, name="gn_sb", tag="gn_sb")
+        nc.gpsimd.dma_start(gn_sb[:], gn.rearrange("(p t) o -> p (t o)", t=PACK))
+        xw = keep.tile([P, T], I32, name="xw", tag="xw")
         nc.sync.dma_start(xw[:], x_words[0].rearrange("p c r -> p (c r)").bitcast(I32))
         tab_sb.append(load_tab(2))
         n1_sb = load_list("n1_sb", n1)
@@ -85,22 +89,17 @@ def tile_picked_layfdifkinda_none_p_kernel(tc, x_words, x_scales, w1, gn, w2, ta
         factor = {}
 
         def fetch_factor(t, hf, tag):
-            tile = keep.tile([P, HALF], F32, name=f"factor{t}{hf}", tag=tag)
+            tile = keep.tile([P, HALF], F32, name=f"factor{t}{hf}", tag=tag, align_bytes=64)
             nc.vector.tensor_copy(tile[:], tab_sb[t][:].indirect(half_list(n3_sb, hf)))
             factor[t, hf] = tile
 
         gn_safe = keep.tile([P, PACK], F32, name="gn_safe")
         gn_inv = keep.tile([P, PACK], F32, name="gn_inv")
         x_scale = keep.tile([P, S], U8, name="x_scale", align_bytes=64)
-        for hf in range(2):
-            fetch_factor(0, hf, f"factor0{hf}")
+        for t in range(2):
+            for hf in range(2):
+                fetch_factor(t, hf, f"factor{t}{hf}")
         nc.vector.tensor_copy(x_scale[:], xs[:].indirect(offs_sb[:]))
-        gn_abs = keep.tile([P, PACK], F32, name="gn_abs", tag="xs")
-        nc.vector.scalar_tensor_tensor(gn_abs[:], gn_sb[:], -1.0, gn_sb[:], ALU.mult, ALU.max)
-        fetch_factor(1, 0, "factor10")
-        nc.vector.scalar_tensor_tensor(gn_safe[:], gn_abs[:], SMALLEST_NORMAL, gn_sb[:], ALU.is_lt, ALU.add)
-        fetch_factor(1, 1, "factor11")
-        nc.vector.reciprocal(gn_inv[:], gn_safe[:])
 
         w1_dealt = keep.tile([P, PACK * H], BF16, name="w1_dealt", align_bytes=64)
         for c in range(2):
@@ -113,8 +112,12 @@ def tile_picked_layfdifkinda_none_p_kernel(tc, x_words, x_scales, w1, gn, w2, ta
         for hf in range(2):
             nc.vector.tensor_copy(x_codes[:, half_cols(hf)], xw[:].bitcast(U32).indirect(half_list(offs_sb, hf)))
 
-        for hf in range(2):
-            fetch_factor(2, hf, f"factor2{hf}")
+        gn_abs = keep.tile([P, PACK], F32, name="gn_abs", tag="xw")
+        nc.vector.scalar_tensor_tensor(gn_abs[:], gn_sb[:], -1.0, gn_sb[:], ALU.mult, ALU.max)
+        fetch_factor(2, 0, "factor20")
+        nc.vector.scalar_tensor_tensor(gn_safe[:], gn_abs[:], SMALLEST_NORMAL, gn_sb[:], ALU.is_lt, ALU.add)
+        fetch_factor(2, 1, "factor21")
+        nc.vector.reciprocal(gn_inv[:], gn_safe[:])
 
         def first_product(bank, t, src_cols, dst_cols):
             cols = slice(t * P, (t + 1) * P)
@@ -152,19 +155,20 @@ def tile_picked_layfdifkinda_none_p_kernel(tc, x_words, x_scales, w1, gn, w2, ta
             subtract(t)
 
         th = {}
-        for hf in range(2):
+
+        def squash(hf):
             for t in range(PACK):
-                tile = keep.tile([P, HALF], F32, name=f"th{t}{hf}", tag=f"th{t}{hf}")
+                tile = keep.tile([P, HALF], F32, name=f"th{t}{hf}")
                 nc.scalar.activation(tile[:], diff[t, hf][:], ACT.Tanh, scale=gn_inv[:, t : t + 1])
                 th[t, hf] = tile
 
         w2_dealt = keep.tile([P, PACK * N], BF16, name="w2_dealt", align_bytes=64)
         w2_codes = keep.tile([P, N], U32, name="w2_codes", align_bytes=64)
         w2_scale = keep.tile([P, N], U8, name="w2_scale", align_bytes=64)
-        z32 = [keep.tile([P, PACK, HALF], F32, name=f"z32_{hf}") for hf in range(2)]
-        z16 = [keep.tile([P, PACK * HALF], BF16, name=f"z16_{hf}", align_bytes=64) for hf in range(2)]
-        z_codes = [keep.tile([P, HALF], U32, name=f"z_codes{hf}", align_bytes=64) for hf in range(2)]
-        z_scale = [keep.tile([P, HALF], U8, name=f"z_scale{hf}", align_bytes=64) for hf in range(2)]
+        z32 = [keep.tile([P, PACK, HALF], F32, name=f"z32_{hf}", tag=f"z32_{hf}", align_bytes=64) for hf in range(2)]
+        z16 = [keep.tile([P, PACK * HALF], BF16, name=f"z16_{hf}", tag=f"z16_{hf}", align_bytes=64) for hf in range(2)]
+        z_codes = keep.tile([P, S], U32, name="z_codes", align_bytes=64)
+        z_scale = keep.tile([P, S], U8, name="z_scale", align_bytes=64)
         h_sb = [keep.tile([P, S], F32, name=f"h{t}") for t in range(PACK)]
 
         def make_z(hf):
@@ -178,31 +182,32 @@ def tile_picked_layfdifkinda_none_p_kernel(tc, x_words, x_scales, w1, gn, w2, ta
             )
 
         def quantize_z(hf):
-            nc.vector.quantize_mx(out=z_codes[hf][:].bitcast(FP8X4), scales=z_scale[hf][:], in_=z16[hf][:])
+            nc.vector.quantize_mx(out=z_codes[:, half_cols(hf)].bitcast(FP8X4), scales=z_scale[:, half_cols(hf)], in_=z16[hf][:])
 
-        def second_product(hf):
-            for t in range(PACK):
-                bank = psum.tile([P, S], F32, name=f"h_ps{t}{hf}", tag=f"bank{PACK * (1 - hf) + t}")
-                cols = slice(t * P, (t + 1) * P)
-                nc.tensor.matmul_mx(bank[:, 0:HALF], w2_codes[:, cols].bitcast(FP8X4), w2_scale[:, cols],
-                                    z_codes[hf][:].bitcast(FP8X4), z_scale[hf][:], start=True, stop=True)
-                nc.scalar.copy(h_sb[t][:, half_cols(hf)], bank[:, 0:HALF])
+        def second_product(t, places, tag):
+            bank = psum.tile([P, S], F32, name=f"h_ps{t}", tag=tag)
+            cols = slice(t * P, (t + 1) * P)
+            nc.tensor.matmul_mx(bank[:, places], w2_codes[:, cols].bitcast(FP8X4), w2_scale[:, cols],
+                                z_codes[:, places].bitcast(FP8X4), z_scale[:, places], start=True, stop=True)
+            nc.scalar.copy(h_sb[t][:, places], bank[:, places])
 
-        for part in range(2):
-            deal_weight(w2_dealt, w2_raw[0], 0, part, 2)
+        squash(0)
+        deal_weight(w2_dealt, w2_raw[0], 0, 0, 1)
+        squash(1)
         make_z(0)
+        deal_weight(w2_dealt, w2_raw[1], 1, 0, 1)
         weave_z(0)
-        for part in range(2):
-            deal_weight(w2_dealt, w2_raw[1], 1, part, 2)
         make_z(1)
         weave_z(1)
-        quantize_z(0)
         nc.vector.quantize_mx(out=w2_codes[:].bitcast(FP8X4), scales=w2_scale[:], in_=w2_dealt[:])
-        second_product(0)
-        fetch_factor(3, 0, "th21")
+        quantize_z(0)
         quantize_z(1)
-        fetch_factor(3, 1, "th31")
-        second_product(1)
+        second_product(0, half_cols(0), "bank5")
+        second_product(0, half_cols(1), "bank6")
+        fetch_factor(3, 0, "z16_1")
+        fetch_factor(3, 1, "z32_1")
+        for t in range(1, PACK):
+            second_product(t, slice(0, S), f"bank{t}")
 
         for t in range(PACK):
             prod = [keep.tile([P, HALF], F32, name=f"prod{t}{hf}") for hf in range(2)]

@@ -43,37 +43,34 @@ def tile_picked_layfdifkinda_none_p_kernel(tc, x_words, x_scales, w1, gn, w2, ta
         out_rows = out.rearrange("(p t) j -> t p j", t=PACK)
 
         def load_tab(t):
-            tile = keep.tile([P, S], F32, name=f"tab{t}")
-            nc.sync.dma_start(tile[:], tab_rows[t])
+            wide = t < PACK - 1
+            tile = keep.tile([P, 2 * S if wide else S], F32, name=f"tab{t}")
+            nc.sync.dma_start(tile[:, 0:S], tab_rows[t])
+            if wide:
+                nc.vector.memset(tile[:, S : 2 * S], 0.0)
             return tile
 
-        def load_weight_half(name, w, c):
-            tile = keep.tile([P, PACK, HALF], F32, name=f"{name}_raw{c}")
-            nc.sync.dma_start(tile[:], w.rearrange("(p j) n -> p j n", j=PACK)[:, :, half_cols(c)])
+        def load_weight(name, w):
+            tile = keep.tile([P, PACK, N], F32, name=name)
+            nc.sync.dma_start(tile[:], w.rearrange("(p j) n -> p j n", j=PACK))
             return tile
 
-        def deal_weight(dealt, raw, c, part, parts):
-            width = HALF // PACK // parts
-            m0 = c * HALF // PACK + part * width
-            nc.scalar.copy(
-                out=dealt[:].rearrange("p (t m j) -> p m j t", t=PACK, j=PACK)[:, m0 : m0 + width],
-                in_=raw[:].rearrange("p j (m t) -> p m j t", t=PACK)[:, part * width : (part + 1) * width],
+        def deal_weight(copy, dealt, raw, m0, m1):
+            copy(
+                dealt[:].rearrange("p (t m j) -> p m j t", t=PACK, j=PACK)[:, m0:m1],
+                raw[:].rearrange("p j (m t) -> p m j t", t=PACK)[:, m0:m1],
             )
 
         xs = keep.tile([P, T], U8, name="xs", tag="xs")
         nc.vector.memset(xs[:].bitcast(I32), 0)
 
-        def load_scale_rows(queue, q):
-            queue.dma_start(xs[32 * q : 32 * q + 4, :].bitcast(I32), x_scales[0, 4 * q : 4 * q + 4, :].bitcast(I32))
-
         tab_sb = [load_tab(0)]
         n3_sb = load_list("n3_sb", n3)
-        w1_raw = [load_weight_half("w1", w1, 0)]
         tab_sb.append(load_tab(1))
+        w1_raw = load_weight("w1_raw", w1)
         offs_sb = load_list("offs_sb", offs)
-        for q in range(4):
-            load_scale_rows(nc.sync, q)
-        w1_raw.append(load_weight_half("w1", w1, 1))
+        for r in range(4):
+            nc.sync.dma_start(xs[r:P:32, :].bitcast(I32), x_scales[0, r:16:4, :].bitcast(I32))
         gn_sb = keep.tile([P, PACK], F32, name="gn_sb", tag="gn_sb")
         nc.gpsimd.dma_start(gn_sb[:], gn.rearrange("(p t) o -> p (t o)", t=PACK))
         xw = keep.tile([P, T], I32, name="xw", tag="xw")
@@ -81,29 +78,27 @@ def tile_picked_layfdifkinda_none_p_kernel(tc, x_words, x_scales, w1, gn, w2, ta
         tab_sb.append(load_tab(2))
         n1_sb = load_list("n1_sb", n1)
         n2_sb = load_list("n2_sb", n2)
-        w2_raw = [load_weight_half("w2", w2, c) for c in range(2)]
+        w2_raw = load_weight("w2_raw", w2)
         tab_sb.append(load_tab(3))
         n5_sb = load_list("n5_sb", n5)
         n4_sb = load_list("n4_sb", n4)
 
-        factor = {}
+        h_sb = [keep.tile([P, 2 * S if t < PACK - 1 else S], F32, name=f"h{t}") for t in range(PACK)]
+        factor = [h_sb[(t - 1) % (PACK - 1)][:, S : 2 * S] for t in range(PACK - 1)]
 
-        def fetch_factor(t, hf, tag):
-            tile = keep.tile([P, HALF], F32, name=f"factor{t}{hf}", tag=tag, align_bytes=64)
-            nc.vector.tensor_copy(tile[:], tab_sb[t][:].indirect(half_list(n3_sb, hf)))
-            factor[t, hf] = tile
+        def fetch_factor(t):
+            nc.vector.tensor_copy(factor[t], tab_sb[t][:].indirect(n3_sb[:]))
 
         gn_safe = keep.tile([P, PACK], F32, name="gn_safe")
         gn_inv = keep.tile([P, PACK], F32, name="gn_inv")
         x_scale = keep.tile([P, S], U8, name="x_scale", align_bytes=64)
         for t in range(2):
-            for hf in range(2):
-                fetch_factor(t, hf, f"factor{t}{hf}")
-        nc.vector.tensor_copy(x_scale[:], xs[:].indirect(offs_sb[:]))
+            fetch_factor(t)
 
         w1_dealt = keep.tile([P, PACK * H], BF16, name="w1_dealt", align_bytes=64)
-        for c in range(2):
-            deal_weight(w1_dealt, w1_raw[c], c, 0, 1)
+        deal_weight(nc.scalar.copy, w1_dealt, w1_raw, 0, 96)
+        deal_weight(nc.vector.tensor_copy, w1_dealt, w1_raw, 96, P)
+        nc.vector.tensor_copy(x_scale[:], xs[:].indirect(offs_sb[:]))
         w1_codes = keep.tile([P, H], U32, name="w1_codes", align_bytes=64)
         w1_scale = keep.tile([P, H], U8, name="w1_scale", align_bytes=64)
         nc.vector.quantize_mx(out=w1_codes[:].bitcast(FP8X4), scales=w1_scale[:], in_=w1_dealt[:])
@@ -114,9 +109,8 @@ def tile_picked_layfdifkinda_none_p_kernel(tc, x_words, x_scales, w1, gn, w2, ta
 
         gn_abs = keep.tile([P, PACK], F32, name="gn_abs", tag="xw")
         nc.vector.scalar_tensor_tensor(gn_abs[:], gn_sb[:], -1.0, gn_sb[:], ALU.mult, ALU.max)
-        fetch_factor(2, 0, "factor20")
         nc.vector.scalar_tensor_tensor(gn_safe[:], gn_abs[:], SMALLEST_NORMAL, gn_sb[:], ALU.is_lt, ALU.add)
-        fetch_factor(2, 1, "factor21")
+        fetch_factor(2)
         nc.vector.reciprocal(gn_inv[:], gn_safe[:])
 
         def first_product(bank, t, src_cols, dst_cols):
@@ -126,18 +120,13 @@ def tile_picked_layfdifkinda_none_p_kernel(tc, x_words, x_scales, w1, gn, w2, ta
 
         y_ps = [psum.tile([P, S], F32, name=f"y_ps{t}", tag=f"bank{t}") for t in range(PACK)]
         y_ps_second = psum.tile([P, S], F32, name="y_ps_second", tag="bank4")
-        gy = [keep.tile([P, S], F32, name=f"gy{t}") for t in range(PACK)]
-        plain = [keep.tile([P, S], F32, name=f"gy_plain{t}") for t in range(PACK)]
-        diff = {}
+        gy = [keep.tile([P, 2 * S if t > 0 else S], F32, name=f"gy{t}") for t in range(PACK)]
+        plain_last = keep.tile([P, S], F32, name="plain_last")
+        plain = [gy[t + 1][:, S : 2 * S] for t in range(PACK - 1)] + [plain_last[:]]
+        diff = [keep.tile([P, S], F32, name=f"diff{t}") for t in range(PACK)]
 
         def gain(dst, src, t):
             nc.scalar.activation(dst, src, ACT.Copy, scale=gn_sb[:, t : t + 1])
-
-        def subtract(t):
-            for hf in range(2):
-                d = keep.tile([P, HALF], F32, name=f"diff{t}{hf}")
-                nc.vector.tensor_tensor(d[:], gy[t][:].indirect(half_list(n1_sb, hf)), plain[t][:, half_cols(hf)], ALU.subtract)
-                diff[t, hf] = d
 
         first_product(y_ps[0], 0, half_cols(0), half_cols(0))
         first_product(y_ps[1], 1, half_cols(0), half_cols(0))
@@ -148,18 +137,20 @@ def tile_picked_layfdifkinda_none_p_kernel(tc, x_words, x_scales, w1, gn, w2, ta
         for hf, bank in enumerate((y_ps[0], y_ps_second)):
             gain(gy[0][:, half_cols(hf)], bank[:, half_cols(hf)], 0)
             gain(plain[0][:, half_cols(hf)], bank[:, half_cols(hf)], 0)
-        subtract(0)
+        for hf in range(2):
+            nc.vector.tensor_tensor(diff[0][:, half_cols(hf)], gy[0][:].indirect(half_list(n1_sb, hf)),
+                                    plain[0][:, half_cols(hf)], ALU.subtract)
         for t in range(1, PACK):
-            gain(gy[t][:], y_ps[t][:], t)
-            gain(plain[t][:], y_ps[t][:], t)
-            subtract(t)
+            gain(gy[t][:, 0:S], y_ps[t][:], t)
+            gain(plain[t], y_ps[t][:], t)
+            nc.vector.tensor_tensor(diff[t][:], gy[t][:].indirect(n1_sb[:]), plain[t], ALU.subtract)
 
         th = {}
 
         def squash(hf):
             for t in range(PACK):
                 tile = keep.tile([P, HALF], F32, name=f"th{t}{hf}")
-                nc.scalar.activation(tile[:], diff[t, hf][:], ACT.Tanh, scale=gn_inv[:, t : t + 1])
+                nc.scalar.activation(tile[:], diff[t][:, half_cols(hf)], ACT.Tanh, scale=gn_inv[:, t : t + 1])
                 th[t, hf] = tile
 
         w2_dealt = keep.tile([P, PACK * N], BF16, name="w2_dealt", align_bytes=64)
@@ -169,7 +160,6 @@ def tile_picked_layfdifkinda_none_p_kernel(tc, x_words, x_scales, w1, gn, w2, ta
         z16 = [keep.tile([P, PACK * HALF], BF16, name=f"z16_{hf}", tag=f"z16_{hf}", align_bytes=64) for hf in range(2)]
         z_codes = keep.tile([P, S], U32, name="z_codes", align_bytes=64)
         z_scale = keep.tile([P, S], U8, name="z_scale", align_bytes=64)
-        h_sb = [keep.tile([P, S], F32, name=f"h{t}") for t in range(PACK)]
 
         def make_z(hf):
             for t in range(PACK):
@@ -192,10 +182,10 @@ def tile_picked_layfdifkinda_none_p_kernel(tc, x_words, x_scales, w1, gn, w2, ta
             nc.scalar.copy(h_sb[t][:, places], bank[:, places])
 
         squash(0)
-        deal_weight(w2_dealt, w2_raw[0], 0, 0, 1)
+        deal_weight(nc.scalar.copy, w2_dealt, w2_raw, 0, P // 2)
         squash(1)
         make_z(0)
-        deal_weight(w2_dealt, w2_raw[1], 1, 0, 1)
+        deal_weight(nc.scalar.copy, w2_dealt, w2_raw, P // 2, P)
         weave_z(0)
         make_z(1)
         weave_z(1)
@@ -204,16 +194,34 @@ def tile_picked_layfdifkinda_none_p_kernel(tc, x_words, x_scales, w1, gn, w2, ta
         quantize_z(1)
         second_product(0, half_cols(0), "bank5")
         second_product(0, half_cols(1), "bank6")
-        fetch_factor(3, 0, "z16_1")
-        fetch_factor(3, 1, "z32_1")
+        last = PACK - 1
+        last_factor = []
+        for hf, tag in enumerate(("z16_1", "z32_1")):
+            tile = keep.tile([P, HALF], F32, name=f"last_factor{hf}", tag=tag, align_bytes=64)
+            nc.vector.tensor_copy(tile[:], tab_sb[last][:].indirect(half_list(n3_sb, hf)))
+            last_factor.append(tile)
         for t in range(1, PACK):
             second_product(t, slice(0, S), f"bank{t}")
 
-        for t in range(PACK):
-            prod = [keep.tile([P, HALF], F32, name=f"prod{t}{hf}") for hf in range(2)]
-            res = [keep.tile([P, HALF], F32, name=f"res{t}{hf}") for hf in range(2)]
-            for hf in range(2):
-                nc.vector.tensor_tensor(prod[hf][:], h_sb[t][:].indirect(half_list(n5_sb, hf)), factor[t, hf][:], ALU.mult)
-            for hf in range(2):
-                nc.vector.tensor_tensor(res[hf][:], tab_sb[t][:].indirect(half_list(n4_sb, hf)), prod[hf][:], ALU.add)
-                nc.sync.dma_start(out_rows[t][:, half_cols(hf)], res[hf][:])
+        prod = [keep.tile([P, S], F32, name=f"prod{t}") for t in range(PACK)]
+        res = [keep.tile([P, S], F32, name=f"res{t}") for t in range(PACK)]
+
+        def multiply(t):
+            nc.vector.tensor_tensor(prod[t][:], h_sb[t][:].indirect(n5_sb[:]), factor[t], ALU.mult)
+
+        def finish(t):
+            nc.vector.tensor_tensor(res[t][:], tab_sb[t][:].indirect(n4_sb[:]), prod[t][:], ALU.add)
+            nc.sync.dma_start(out_rows[t], res[t][:])
+
+        multiply(0)
+        for t in range(1, last):
+            multiply(t)
+            finish(t - 1)
+        for hf in range(2):
+            nc.vector.tensor_tensor(prod[last][:, half_cols(hf)], h_sb[last][:].indirect(half_list(n5_sb, hf)),
+                                    last_factor[hf][:], ALU.mult)
+        finish(last - 1)
+        for j0, j1 in ((0, 256), (256, 384), (384, 512)):
+            nc.vector.tensor_tensor(res[last][:, j0:j1], tab_sb[last][:].indirect(n4_sb[:, j0 // 16 : j1 // 16]),
+                                    prod[last][:, j0:j1], ALU.add)
+            nc.sync.dma_start(out_rows[last][:, j0:j1], res[last][:, j0:j1])

from contextlib import ExitStack

import concourse.mybir as mybir

K, T, S, N, H = 512, 2048, 512, 512, 512
FLOPS = 2 * K * H * S + 2 * H * N * S

F32 = mybir.dt.float32
BF16 = mybir.dt.bfloat16
I32 = mybir.dt.int32
U32 = mybir.dt.uint32
U16 = mybir.dt.uint16
U8 = mybir.dt.uint8
FP8X4 = mybir.dt.float8_e4m3fn_x4
ALU = mybir.AluOpType
ACT = mybir.ActivationFunctionType

P = 128
PACK = 4
HALF = S // 2
LIST_COLS = S // 16
SMALLEST_NORMAL = 2.0 ** -126


def tile_picked_layfdifkinda_none_p_kernel(tc, x_words, x_scales, w1, gn, w2, tab, offs, n1, n2, n3, n4, n5, out):
    nc = tc.nc
    with ExitStack() as ctx:
        keep = ctx.enter_context(tc.tile_pool(name="keep", bufs=1))
        psum = ctx.enter_context(tc.psum_pool(name="psum", bufs=1))

        def load_list(name, src):
            tile = keep.tile([P, LIST_COLS], U16, name=name)
            nc.sync.dma_start(tile[:], src)
            return tile

        def half_cols(hf):
            return slice(hf * HALF, (hf + 1) * HALF)

        def half_list(tile, hf):
            return tile[:, hf * LIST_COLS // 2 : (hf + 1) * LIST_COLS // 2]

        tab_rows = tab.rearrange("(p t) j -> t p j", t=PACK)
        out_rows = out.rearrange("(p t) j -> t p j", t=PACK)

        def load_tab(t):
            wide = t < PACK - 1
            tile = keep.tile([P, 2 * S if wide else S], F32, name=f"tab{t}")
            nc.sync.dma_start(tile[:, 0:S], tab_rows[t])
            if wide:
                nc.vector.memset(tile[:, S : 2 * S], 0.0)
            return tile

        def load_weight(name, w):
            tile = keep.tile([P, PACK, N], F32, name=name)
            nc.sync.dma_start(tile[:], w.rearrange("(p j) n -> p j n", j=PACK))
            return tile

        def deal_weight(copy, dealt, raw, m0, m1):
            copy(
                dealt[:].rearrange("p (t m j) -> p m j t", t=PACK, j=PACK)[:, m0:m1],
                raw[:].rearrange("p j (m t) -> p m j t", t=PACK)[:, m0:m1],
            )

        xs = keep.tile([P, T], U8, name="xs", tag="xs")
        nc.vector.memset(xs[:].bitcast(I32), 0)

        tab_sb = [load_tab(0)]
        n3_sb = load_list("n3_sb", n3)
        tab_sb.append(load_tab(1))
        w1_raw = load_weight("w1_raw", w1)
        offs_sb = load_list("offs_sb", offs)
        for r in range(4):
            nc.sync.dma_start(xs[r:P:32, :].bitcast(I32), x_scales[0, r:16:4, :].bitcast(I32))
        gn_sb = keep.tile([P, PACK], F32, name="gn_sb", tag="gn_sb")
        nc.gpsimd.dma_start(gn_sb[:], gn.rearrange("(p t) o -> p (t o)", t=PACK))
        xw = keep.tile([P, T], I32, name="xw", tag="xw")
        nc.sync.dma_start(xw[:], x_words[0].rearrange("p c r -> p (c r)").bitcast(I32))
        tab_sb.append(load_tab(2))
        n1_sb = load_list("n1_sb", n1)
        n2_sb = load_list("n2_sb", n2)
        w2_raw = load_weight("w2_raw", w2)
        tab_sb.append(load_tab(3))
        n5_sb = load_list("n5_sb", n5)
        n4_sb = load_list("n4_sb", n4)

        h_sb = [keep.tile([P, 2 * S if t < PACK - 1 else S], F32, name=f"h{t}") for t in range(PACK)]
        factor = [h_sb[(t - 1) % (PACK - 1)][:, S : 2 * S] for t in range(PACK - 1)]

        def fetch_factor(t):
            nc.vector.tensor_copy(factor[t], tab_sb[t][:].indirect(n3_sb[:]))

        gn_safe = keep.tile([P, PACK], F32, name="gn_safe")
        gn_inv = keep.tile([P, PACK], F32, name="gn_inv")
        x_scale = keep.tile([P, S], U8, name="x_scale", align_bytes=64)
        for t in range(2):
            fetch_factor(t)

        w1_dealt = keep.tile([P, PACK * H], BF16, name="w1_dealt", align_bytes=64)
        deal_weight(nc.scalar.copy, w1_dealt, w1_raw, 0, 96)
        deal_weight(nc.vector.tensor_copy, w1_dealt, w1_raw, 96, P)
        nc.vector.tensor_copy(x_scale[:], xs[:].indirect(offs_sb[:]))
        w1_codes = keep.tile([P, H], U32, name="w1_codes", align_bytes=64)
        w1_scale = keep.tile([P, H], U8, name="w1_scale", align_bytes=64)
        nc.vector.quantize_mx(out=w1_codes[:].bitcast(FP8X4), scales=w1_scale[:], in_=w1_dealt[:])

        x_codes = keep.tile([P, S], U32, name="x_codes", align_bytes=64)
        for hf in range(2):
            nc.vector.tensor_copy(x_codes[:, half_cols(hf)], xw[:].bitcast(U32).indirect(half_list(offs_sb, hf)))

        gn_abs = keep.tile([P, PACK], F32, name="gn_abs", tag="xw")
        nc.vector.scalar_tensor_tensor(gn_abs[:], gn_sb[:], -1.0, gn_sb[:], ALU.mult, ALU.max)
        nc.vector.scalar_tensor_tensor(gn_safe[:], gn_abs[:], SMALLEST_NORMAL, gn_sb[:], ALU.is_lt, ALU.add)
        fetch_factor(2)
        nc.vector.reciprocal(gn_inv[:], gn_safe[:])

        def first_product(bank, t, src_cols, dst_cols):
            cols = slice(t * P, (t + 1) * P)
            nc.tensor.matmul_mx(bank[:, dst_cols], w1_codes[:, cols].bitcast(FP8X4), w1_scale[:, cols],
                                x_codes[:, src_cols].bitcast(FP8X4), x_scale[:, src_cols], start=True, stop=True)

        y_ps = [psum.tile([P, S], F32, name=f"y_ps{t}", tag=f"bank{t}") for t in range(PACK)]
        y_ps_second = psum.tile([P, S], F32, name="y_ps_second", tag="bank4")
        gy = [keep.tile([P, 2 * S if t > 0 else S], F32, name=f"gy{t}") for t in range(PACK)]
        plain_last = keep.tile([P, S], F32, name="plain_last")
        plain = [gy[t + 1][:, S : 2 * S] for t in range(PACK - 1)] + [plain_last[:]]
        diff = [keep.tile([P, S], F32, name=f"diff{t}") for t in range(PACK)]

        def gain(dst, src, t):
            nc.scalar.activation(dst, src, ACT.Copy, scale=gn_sb[:, t : t + 1])

        first_product(y_ps[0], 0, half_cols(0), half_cols(0))
        first_product(y_ps[1], 1, half_cols(0), half_cols(0))
        first_product(y_ps_second, 0, half_cols(1), half_cols(1))
        first_product(y_ps[1], 1, half_cols(1), half_cols(1))
        for t in range(2, PACK):
            first_product(y_ps[t], t, slice(0, S), slice(0, S))
        for hf, bank in enumerate((y_ps[0], y_ps_second)):
            gain(gy[0][:, half_cols(hf)], bank[:, half_cols(hf)], 0)
            gain(plain[0][:, half_cols(hf)], bank[:, half_cols(hf)], 0)
        for hf in range(2):
            nc.vector.tensor_tensor(diff[0][:, half_cols(hf)], gy[0][:].indirect(half_list(n1_sb, hf)),
                                    plain[0][:, half_cols(hf)], ALU.subtract)
        for t in range(1, PACK):
            gain(gy[t][:, 0:S], y_ps[t][:], t)
            gain(plain[t], y_ps[t][:], t)
            nc.vector.tensor_tensor(diff[t][:], gy[t][:].indirect(n1_sb[:]), plain[t], ALU.subtract)

        th = {}

        def squash(hf):
            for t in range(PACK):
                tile = keep.tile([P, HALF], F32, name=f"th{t}{hf}")
                nc.scalar.activation(tile[:], diff[t][:, half_cols(hf)], ACT.Tanh, scale=gn_inv[:, t : t + 1])
                th[t, hf] = tile

        w2_dealt = keep.tile([P, PACK * N], BF16, name="w2_dealt", align_bytes=64)
        w2_codes = keep.tile([P, N], U32, name="w2_codes", align_bytes=64)
        w2_scale = keep.tile([P, N], U8, name="w2_scale", align_bytes=64)
        z32 = [keep.tile([P, PACK, HALF], F32, name=f"z32_{hf}", tag=f"z32_{hf}", align_bytes=64) for hf in range(2)]
        z16 = [keep.tile([P, PACK * HALF], BF16, name=f"z16_{hf}", tag=f"z16_{hf}", align_bytes=64) for hf in range(2)]
        z_codes = keep.tile([P, S], U32, name="z_codes", align_bytes=64)
        z_scale = keep.tile([P, S], U8, name="z_scale", align_bytes=64)

        def make_z(hf):
            for t in range(PACK):
                nc.vector.tensor_tensor(z32[hf][:, t, :], gy[t][:].indirect(half_list(n2_sb, hf)), th[t, hf][:], ALU.mult)

        def weave_z(hf):
            nc.scalar.copy(
                out=z16[hf][:].rearrange("p (c i t) -> p c t i", i=4, t=PACK),
                in_=z32[hf][:].rearrange("p t (c i) -> p c t i", i=4),
            )

        def quantize_z(hf):
            nc.vector.quantize_mx(out=z_codes[:, half_cols(hf)].bitcast(FP8X4), scales=z_scale[:, half_cols(hf)], in_=z16[hf][:])

        def second_product(t, places, tag):
            bank = psum.tile([P, S], F32, name=f"h_ps{t}", tag=tag)
            cols = slice(t * P, (t + 1) * P)
            nc.tensor.matmul_mx(bank[:, places], w2_codes[:, cols].bitcast(FP8X4), w2_scale[:, cols],
                                z_codes[:, places].bitcast(FP8X4), z_scale[:, places], start=True, stop=True)
            nc.scalar.copy(h_sb[t][:, places], bank[:, places])

        squash(0)
        deal_weight(nc.scalar.copy, w2_dealt, w2_raw, 0, P // 2)
        squash(1)
        make_z(0)
        deal_weight(nc.scalar.copy, w2_dealt, w2_raw, P // 2, P)
        weave_z(0)
        make_z(1)
        weave_z(1)
        nc.vector.quantize_mx(out=w2_codes[:].bitcast(FP8X4), scales=w2_scale[:], in_=w2_dealt[:])
        quantize_z(0)
        quantize_z(1)
        second_product(0, half_cols(0), "bank5")
        second_product(0, half_cols(1), "bank6")
        last = PACK - 1
        last_factor = []
        for hf, tag in enumerate(("z16_1", "z32_1")):
            tile = keep.tile([P, HALF], F32, name=f"last_factor{hf}", tag=tag, align_bytes=64)
            nc.vector.tensor_copy(tile[:], tab_sb[last][:].indirect(half_list(n3_sb, hf)))
            last_factor.append(tile)
        for t in range(1, PACK):
            second_product(t, slice(0, S), f"bank{t}")

        prod = [keep.tile([P, S], F32, name=f"prod{t}") for t in range(PACK)]
        res = [keep.tile([P, S], F32, name=f"res{t}") for t in range(PACK)]

        def multiply(t):
            nc.vector.tensor_tensor(prod[t][:], h_sb[t][:].indirect(n5_sb[:]), factor[t], ALU.mult)

        def finish(t):
            nc.vector.tensor_tensor(res[t][:], tab_sb[t][:].indirect(n4_sb[:]), prod[t][:], ALU.add)
            nc.sync.dma_start(out_rows[t], res[t][:])

        multiply(0)
        for t in range(1, last):
            multiply(t)
            finish(t - 1)
        for hf in range(2):
            nc.vector.tensor_tensor(prod[last][:, half_cols(hf)], h_sb[last][:].indirect(half_list(n5_sb, hf)),
                                    last_factor[hf][:], ALU.mult)
        finish(last - 1)
        for j0, j1 in ((0, 256), (256, 384), (384, 512)):
            nc.vector.tensor_tensor(res[last][:, j0:j1], tab_sb[last][:].indirect(n4_sb[:, j0 // 16 : j1 // 16]),
                                    prod[last][:, j0:j1], ALU.add)
            nc.sync.dma_start(out_rows[last][:, j0:j1], res[last][:, j0:j1])
